import numpy as np
import ml_dtypes


def mxq(x, axis, fmt="e4m3"):
    dtype, down = {"e4m3": (ml_dtypes.float8_e4m3fn, 7), "e5m2": (ml_dtypes.float8_e5m2, 14)}[fmt]
    v = np.moveaxis(np.asarray(x, np.float32).astype(ml_dtypes.bfloat16).astype(np.float64), axis, -1)
    blocks = v.reshape(v.shape[:-1] + (-1, 32))
    amax = np.abs(blocks).max(-1, keepdims=True)
    byte = np.maximum(np.where(amax > 0, np.frexp(amax)[1] - 1 + 127, 0) - down, 1)
    scale = np.exp2(byte - 127.0)
    codes = (blocks / scale).astype(np.float32).astype(dtype).astype(np.float64)
    return np.moveaxis((codes * scale).reshape(v.shape), -1, axis)


WIDE = False


def mx_kscale(k):
    if not WIDE:
        return np.ones(k)
    levels = np.array([10, -10, 5, -5, 0])
    if k % 512:
        return np.exp2(np.random.permutation(np.resize(levels, k // 32))).repeat(32)
    a = np.empty((k // 512, 16))
    for p in range(k // 512):
        a[p, :8] = np.random.permutation(np.resize(levels, 8))
        for g in range(8):
            far = levels[np.abs(levels - a[p, g]) >= 10]
            a[p, g + 8] = far[np.random.randint(len(far))]
    return np.exp2(a.ravel()).repeat(32)


def f64(x):
    return np.asarray(x).astype(np.float64)


def striped8(idx):
    return np.asarray(idx).reshape(8, -1, 16).transpose(0, 2, 1).reshape(128, -1).astype(np.uint16)


def unstriped8(offs):
    return offs.reshape(8, 16, -1).transpose(0, 2, 1).reshape(8, -1).astype(np.int64)


def pick8(x, idx, run):
    r = np.arange(len(x))
    return x[r[:, None], idx[r % (8 * run) // run]]


E2M1 = np.array([0.0, 0.5, 1.0, 1.5, 2.0, 3.0, 4.0, 6.0, -0.0, -0.5, -1.0, -1.5, -2.0, -3.0, -4.0, -6.0])


def pack_weight(w, fmt):
    k, n = w.shape
    w = f64(np.asarray(w, np.float32).astype(ml_dtypes.bfloat16)).reshape(k // 32, 32, n)
    amax = np.abs(w).max(1)
    if fmt == "e4m3":
        byte = np.frexp(amax)[1] - 1 + 127 - 7
    else:
        mant, ex = np.frexp(amax / 6.0)
        byte = np.where(mant > 0.5, ex, ex - 1) + 127
    byte = np.clip(np.where(amax > 0, byte, 1), 1, 254)
    scaled = (w * np.exp2(127.0 - byte)[:, None, :]).reshape(k, n).astype(np.float32)
    by_word = np.ascontiguousarray(scaled.reshape(k // 512, 128, 4, n).transpose(0, 1, 3, 2))
    if fmt == "e4m3":
        words = by_word.astype(ml_dtypes.float8_e4m3fn).view(np.uint8)
    else:
        c = by_word.astype(ml_dtypes.float4_e2m1fn).view(np.uint8) & 0xF
        words = (c[..., 0::2] | (c[..., 1::2] << 4)).reshape(k // 512, 128, 2 * n)
    return np.ascontiguousarray(words), np.ascontiguousarray(byte.astype(np.uint8).reshape(k // 512, 16, n))


def unpack_weight(words, scales, fmt):
    g, _, n = scales.shape
    words = np.ascontiguousarray(words).reshape(g, 128, n, -1)
    if fmt == "e4m3":
        vals = words.view(ml_dtypes.float8_e4m3fn).astype(np.float64)
    else:
        nib = np.empty((g, 128, n, 4), np.uint8)
        nib[..., 0::2] = words & 0xF
        nib[..., 1::2] = words >> 4
        vals = E2M1[nib]
    vals = vals * np.repeat(np.exp2(scales.astype(np.float64) - 127.0), 8, axis=1)[..., None]
    return vals.transpose(0, 1, 3, 2).reshape(g * 512, n)


D, T, U, X, Z, I, J, M, Q = 512, 1024, 512, 512, 1024, 512, 256, 128, 128


def setup_inputs():
    n = np.random.standard_normal
    idx = np.stack([np.random.permutation(T)[:J] for _ in range(8)])
    idx2 = np.stack([np.random.permutation(U)[:M] for _ in range(8)])
    idx3 = np.stack([np.random.permutation(X)[:M] for _ in range(8)])
    idx4 = np.stack([np.random.permutation(Z)[:I] for _ in range(8)])
    idx5 = np.stack([np.random.permutation(Z)[:I] for _ in range(8)])
    fd = mx_kscale(D)
    cachep = pack_weight(n((D, T)) / fd[:, None], "e2m1")
    draftp = pack_weight(n((D, U)) / fd[:, None], "e4m3")
    archp = pack_weight(n((D, X)) / fd[:, None], "e2m1")
    return {
        "query": (n((D, Q)) * 1.0 / np.sqrt(D) * fd[:, None]).astype(np.float32),
        "cache_words": cachep[0],
        "cache_scales": cachep[1],
        "draft_words": draftp[0],
        "draft_scales": draftp[1],
        "arch_words": archp[0],
        "arch_scales": archp[1],
        "offs": striped8(idx),
        "offs2": striped8(idx2),
        "offs3": striped8(idx3),
        "offs4": striped8(idx4),
        "offs5": striped8(idx5),
    }


def reference(query, cache_words, cache_scales, draft_words, draft_scales, arch_words, arch_scales, offs, offs2, offs3, offs4, offs5):
    idx = unstriped8(offs)
    idx2 = unstriped8(offs2)
    idx3 = unstriped8(offs3)
    idx4 = unstriped8(offs4)
    idx5 = unstriped8(offs5)
    cacheu = unpack_weight(cache_words, cache_scales, "e2m1")
    draftu = unpack_weight(draft_words, draft_scales, "e4m3")
    archu = unpack_weight(arch_words, arch_scales, "e2m1")
    queryq = mxq(f64(query), 0, "e4m3")
    a = queryq.T @ cacheu
    b = queryq.T @ draftu
    c0 = queryq.T @ archu
    v = np.concatenate([pick8(b, idx2, 16), pick8(c0, idx3, 16)], axis=1)
    w = np.concatenate([pick8(a, idx, 16), v], axis=1)
    f1 = np.zeros((Q, Z))
    f1[np.arange(Q)[:, None], idx4[np.arange(Q) % 128 // 16]] = w
    y = np.maximum(pick8(f1, idx5, 16), w)
    return y

@@ -1,0 +1,128 @@
+from contextlib import ExitStack
+
+import concourse.mybir as mybir
+
+F32 = mybir.dt.float32
+BF16 = mybir.dt.bfloat16
+I32 = mybir.dt.int32
+U32 = mybir.dt.uint32
+U16 = mybir.dt.uint16
+U8 = mybir.dt.uint8
+FP8X4 = mybir.dt.float8_e4m3fn_x4
+FP4X4 = mybir.dt.float4_e2m1fn_x4
+COPY = mybir.ActivationFunctionType.Copy
+MAX = mybir.AluOpType.max
+
+P = 128
+D, Q = 512, 128
+T, U, X, Z = 1024, 512, 512, 1024
+SLOTS = 512
+N = 256
+FLOPS = 2 * D * Q * (T + U + X)
+
+
+def tile_attend_raggedthree_three_kernel(tc, query, cache_words, cache_scales, draft_words, draft_scales,
+                                          arch_words, arch_scales, offs, offs2, offs3, offs4, offs5, out):
+    nc = tc.nc
+    with ExitStack() as ctx:
+        lists = ctx.enter_context(tc.tile_pool(name="lists", bufs=1))
+        keep = ctx.enter_context(tc.tile_pool(name="keep", bufs=1))
+        psum = ctx.enter_context(tc.psum_pool(name="psum", bufs=1))
+
+        def load_list(name, src):
+            tile = lists.tile(list(src.shape), U16, name=name)
+            nc.sync.dma_start(tile[:], src)
+            return tile
+
+        def scale_tile(name, width):
+            plane = keep.tile([P, 2, width], U8, name=name, align_bytes=64)
+            nc.vector.memset(plane[:, 0, :].bitcast(I32), 0)
+            return plane
+
+        def load_scales(plane, src, h, queue):
+            queue.dma_start(plane[64 * h : 64 * h + 4, :, :].bitcast(I32),
+                            src[0, 8 * h : 8 * h + 8, :].bitcast(I32).rearrange("(g r) n -> r g n", r=4))
+
+        def load_words(name, src, nbytes):
+            words = keep.tile([P, nbytes], U8, name=name, align_bytes=64)
+            nc.sync.dma_start(words[:].bitcast(I32), src.bitcast(I32))
+            return words
+
+        q_raw = keep.tile([P, 4, Q], F32)
+        nc.sync.dma_start(q_raw[:], query.rearrange("(p j) q -> p j q", j=4))
+        arch_s = scale_tile("arch_s", X)
+        draft_s = scale_tile("draft_s", U)
+        cache_s = scale_tile("cache_s", T)
+        for plane, src in ((arch_s, arch_scales), (draft_s, draft_scales)):
+            for h in range(2):
+                load_scales(plane, src, h, nc.scalar)
+        arch_w = load_words("arch_w", arch_words[0], 2 * X)
+        draft_w = load_words("draft_w", draft_words[0].rearrange("p n t -> p (n t)"), 4 * U)
+        cache_w = load_words("cache_w", cache_words[0], 2 * T)
+        load_scales(cache_s, cache_scales, 0, nc.sync)
+        arch_list = load_list("arch_list", offs3)
+        load_scales(cache_s, cache_scales, 1, nc.sync)
+        put_list = load_list("put_list", offs4)
+        draft_list = load_list("draft_list", offs2)
+        cache_list = load_list("cache_list", offs)
+        get_list = load_list("get_list", offs5)
+
+        page = keep.tile([P, Z], F32)
+        nc.vector.memset(page[:], 0.0)
+
+        def spread_scales(plane):
+            for h in range(2):
+                nc.vector.tensor_copy(plane[64 * h + 32 : 64 * h + 36, 0, :].bitcast(I32),
+                                      plane[64 * h : 64 * h + 4, 1, :].bitcast(I32))
+
+        q_bf = keep.tile([P, Q, 4], BF16, align_bytes=64)
+        nc.vector.tensor_copy(q_bf[:], q_raw[:].rearrange("p j q -> p q j"))
+        spread_scales(arch_s)
+        q_codes = keep.tile([P, Q], U32, align_bytes=64)
+        q_scales = keep.tile([P, Q], U8, align_bytes=64)
+        nc.vector.quantize_mx(out=q_codes[:].bitcast(FP8X4), scales=q_scales[:],
+                              in_=q_bf[:].rearrange("p q j -> p (q j)"))
+        spread_scales(draft_s)
+        spread_scales(cache_s)
+
+        def scores(res, first, words, plane, dtype, on_scalar):
+            per = words.shape[1] // 512
+            for c in range(2):
+                cols = slice(first + N * c, first + N * (c + 1))
+                bank = psum.tile([P, N], F32, name="bank", bufs=8)
+                nc.tensor.matmul_mx(out=bank[:], lhsT=q_codes[:].bitcast(FP8X4), lhsT_scale=q_scales[:],
+                                    rhs=words[:, per * N * c : per * N * (c + 1)].bitcast(dtype),
+                                    rhs_scale=plane[:, 0, cols], start=True, stop=True)
+                if on_scalar[c]:
+                    nc.scalar.activation(res[:, cols], bank[:], COPY)
+                else:
+                    nc.vector.tensor_copy(res[:, cols], bank[:])
+
+        w = keep.tile([P, SLOTS], F32)
+
+        def pick_and_put(res, offsets, first):
+            n = 16 * offsets.shape[1]
+            nc.vector.tensor_copy(w[:, first : first + n], res[:].indirect(offsets[:]))
+            nc.scalar.activation(page[:].indirect(put_list[:, first // 16 : (first + n) // 16]),
+                                 w[:, first : first + n], COPY)
+
+        c0 = keep.tile([P, X], F32)
+        a = keep.tile([P, T], F32)
+        b = keep.tile([P, U], F32)
+        scores(c0, 0, arch_w, arch_s, FP4X4, (True, True))
+        scores(b, 0, draft_w, draft_s, FP8X4, (True, True))
+        pick_and_put(c0, arch_list, 384)
+        scores(a, 0, cache_w[:, :T], cache_s, FP4X4, (False, False))
+        scores(a, 512, cache_w[:, T:], cache_s, FP4X4, (False, True))
+        pick_and_put(b, draft_list, 256)
+        pick_and_put(a, cache_list, 0)
+
+        half = SLOTS // 2
+        got = keep.tile([P, SLOTS], F32)
+        res = keep.tile([P, SLOTS], F32)
+        nc.vector.tensor_copy(got[:, :half], page[:].indirect(get_list[:, : half // 16]))
+        nc.scalar.activation(got[:, half:], page[:].indirect(get_list[:, half // 16 :]), COPY)
+        for h in range(2):
+            cols = slice(h * half, (h + 1) * half)
+            nc.vector.tensor_tensor(res[:, cols], got[:, cols], w[:, cols], MAX)
+            nc.sync.dma_start(out[:, cols], res[:, cols])

@@ -34,14 +34,16 @@ def tile_attend_raggedthree_three_kernel(tc, query, cache_words, cache_scales, d
             nc.sync.dma_start(tile[:], src)
             return tile
 
-        def scale_tile(name, width):
-            plane = keep.tile([P, 2, width], U8, name=name, align_bytes=64)
+        def scale_tile(name, width, loads):
+            plane = keep.tile([P, 4 // loads, width], U8, name=name, align_bytes=64)
             nc.vector.memset(plane[:, 0, :].bitcast(I32), 0)
             return plane
 
-        def load_scales(plane, src, h, queue):
-            queue.dma_start(plane[64 * h : 64 * h + 4, :, :].bitcast(I32),
-                            src[0, 8 * h : 8 * h + 8, :].bitcast(I32).rearrange("(g r) n -> r g n", r=4))
+        def load_scales(plane, src):
+            groups = plane.shape[1]
+            for first in range(0, 4, groups):
+                nc.sync.dma_start(plane[32 * first : 32 * first + 4, :, :].bitcast(I32),
+                                  src[0, 4 * first : 4 * (first + groups), :].bitcast(I32).rearrange("(g r) n -> r g n", r=4))
 
         def load_words(name, src, nbytes):
             words = keep.tile([P, nbytes], U8, name=name, align_bytes=64)
@@ -50,20 +52,18 @@ def tile_attend_raggedthree_three_kernel(tc, query, cache_words, cache_scales, d
 
         q_raw = keep.tile([P, 4, Q], F32)
         nc.sync.dma_start(q_raw[:], query.rearrange("(p j) q -> p j q", j=4))
-        arch_s = scale_tile("arch_s", X)
-        draft_s = scale_tile("draft_s", U)
-        cache_s = scale_tile("cache_s", T)
-        for plane, src in ((arch_s, arch_scales), (draft_s, draft_scales)):
-            for h in range(2):
-                load_scales(plane, src, h, nc.scalar)
+        arch_s = scale_tile("arch_s", X, 2)
+        draft_s = scale_tile("draft_s", U, 1)
+        cache_s = scale_tile("cache_s", T, 1)
+        load_scales(arch_s, arch_scales)
         arch_w = load_words("arch_w", arch_words[0], 2 * X)
+        load_scales(draft_s, draft_scales)
         draft_w = load_words("draft_w", draft_words[0].rearrange("p n t -> p (n t)"), 4 * U)
+        load_scales(cache_s, cache_scales)
         cache_w = load_words("cache_w", cache_words[0], 2 * T)
-        load_scales(cache_s, cache_scales, 0, nc.sync)
         arch_list = load_list("arch_list", offs3)
-        load_scales(cache_s, cache_scales, 1, nc.sync)
-        put_list = load_list("put_list", offs4)
         draft_list = load_list("draft_list", offs2)
+        put_list = load_list("put_list", offs4)
         cache_list = load_list("cache_list", offs)
         get_list = load_list("get_list", offs5)
 
@@ -71,12 +71,15 @@ def tile_attend_raggedthree_three_kernel(tc, query, cache_words, cache_scales, d
         nc.vector.memset(page[:], 0.0)
 
         def spread_scales(plane):
-            for h in range(2):
-                nc.vector.tensor_copy(plane[64 * h + 32 : 64 * h + 36, 0, :].bitcast(I32),
-                                      plane[64 * h : 64 * h + 4, 1, :].bitcast(I32))
+            groups = plane.shape[1]
+            for first in range(0, 4, groups):
+                for g in range(1, groups):
+                    nc.vector.tensor_copy(plane[32 * (first + g) : 32 * (first + g) + 4, 0, :].bitcast(I32),
+                                          plane[32 * first : 32 * first + 4, g, :].bitcast(I32))
 
         q_bf = keep.tile([P, Q, 4], BF16, align_bytes=64)
-        nc.vector.tensor_copy(q_bf[:], q_raw[:].rearrange("p j q -> p q j"))
+        nc.vector.tensor_copy(q_bf[:].rearrange("p (c i) j -> p c j i", i=4),
+                              q_raw[:].rearrange("p j (c i) -> p c j i", i=4))
         spread_scales(arch_s)
         q_codes = keep.tile([P, Q], U32, align_bytes=64)
         q_scales = keep.tile([P, Q], U8, align_bytes=64)
@@ -113,7 +116,7 @@ def tile_attend_raggedthree_three_kernel(tc, query, cache_words, cache_scales, d
         scores(b, 0, draft_w, draft_s, FP8X4, (True, True))
         pick_and_put(c0, arch_list, 384)
         scores(a, 0, cache_w[:, :T], cache_s, FP4X4, (False, False))
-        scores(a, 512, cache_w[:, T:], cache_s, FP4X4, (False, True))
+        scores(a, 512, cache_w[:, T:], cache_s, FP4X4, (False, False))
         pick_and_put(b, draft_list, 256)
         pick_and_put(a, cache_list, 0)
 

@@ -39,11 +39,10 @@ def tile_attend_raggedthree_three_kernel(tc, query, cache_words, cache_scales, d
             nc.vector.memset(plane[:, 0, :].bitcast(I32), 0)
             return plane
 
-        def load_scales(plane, src):
+        def load_scales(plane, src, first, queue):
             groups = plane.shape[1]
-            for first in range(0, 4, groups):
-                nc.sync.dma_start(plane[32 * first : 32 * first + 4, :, :].bitcast(I32),
-                                  src[0, 4 * first : 4 * (first + groups), :].bitcast(I32).rearrange("(g r) n -> r g n", r=4))
+            queue.dma_start(plane[32 * first : 32 * first + 4, :, :].bitcast(I32),
+                            src[0, 4 * first : 4 * (first + groups), :].bitcast(I32).rearrange("(g r) n -> r g n", r=4))
 
         def load_words(name, src, nbytes):
             words = keep.tile([P, nbytes], U8, name=name, align_bytes=64)
@@ -52,19 +51,22 @@ def tile_attend_raggedthree_three_kernel(tc, query, cache_words, cache_scales, d
 
         q_raw = keep.tile([P, 4, Q], F32)
         nc.sync.dma_start(q_raw[:], query.rearrange("(p j) q -> p j q", j=4))
-        arch_s = scale_tile("arch_s", X, 2)
-        draft_s = scale_tile("draft_s", U, 1)
-        cache_s = scale_tile("cache_s", T, 1)
-        load_scales(arch_s, arch_scales)
-        arch_w = load_words("arch_w", arch_words[0], 2 * X)
-        load_scales(draft_s, draft_scales)
-        draft_w = load_words("draft_w", draft_words[0].rearrange("p n t -> p (n t)"), 4 * U)
-        load_scales(cache_s, cache_scales)
+        cache_s = scale_tile("cache_s", T, 4)
+        draft_s = scale_tile("draft_s", U, 2)
+        arch_s = scale_tile("arch_s", X, 4)
+        for g in range(4):
+            load_scales(cache_s, cache_scales, g, nc.scalar)
         cache_w = load_words("cache_w", cache_words[0], 2 * T)
-        arch_list = load_list("arch_list", offs3)
-        draft_list = load_list("draft_list", offs2)
-        put_list = load_list("put_list", offs4)
+        for g in (0, 2):
+            load_scales(draft_s, draft_scales, g, nc.sync)
         cache_list = load_list("cache_list", offs)
+        draft_w = load_words("draft_w", draft_words[0].rearrange("p n t -> p (n t)"), 4 * U)
+        arch_w = load_words("arch_w", arch_words[0], 2 * X)
+        for g in range(4):
+            load_scales(arch_s, arch_scales, g, nc.sync)
+        put_list = load_list("put_list", offs4)
+        draft_list = load_list("draft_list", offs2)
+        arch_list = load_list("arch_list", offs3)
         get_list = load_list("get_list", offs5)
 
         page = keep.tile([P, Z], F32)
@@ -78,47 +80,52 @@ def tile_attend_raggedthree_three_kernel(tc, query, cache_words, cache_scales, d
                                           plane[32 * first : 32 * first + 4, g, :].bitcast(I32))
 
         q_bf = keep.tile([P, Q, 4], BF16, align_bytes=64)
-        nc.vector.tensor_copy(q_bf[:].rearrange("p (c i) j -> p c j i", i=4),
-                              q_raw[:].rearrange("p j (c i) -> p c j i", i=4))
-        spread_scales(arch_s)
         q_codes = keep.tile([P, Q], U32, align_bytes=64)
         q_scales = keep.tile([P, Q], U8, align_bytes=64)
-        nc.vector.quantize_mx(out=q_codes[:].bitcast(FP8X4), scales=q_scales[:],
-                              in_=q_bf[:].rearrange("p q j -> p (q j)"))
+        q_halves = (slice(0, Q // 2), slice(Q // 2, Q))
+        for rows in q_halves:
+            nc.vector.tensor_copy(q_bf[:, rows, :].rearrange("p (c i) j -> p c j i", i=4),
+                                  q_raw[:, :, rows].rearrange("p j (c i) -> p c j i", i=4))
+        for rows in q_halves:
+            nc.vector.quantize_mx(out=q_codes[:, rows].bitcast(FP8X4), scales=q_scales[:, rows],
+                                  in_=q_bf[:, rows, :].rearrange("p q j -> p (q j)"))
         spread_scales(draft_s)
-        spread_scales(cache_s)
 
-        def scores(res, first, words, plane, dtype, on_scalar):
-            per = words.shape[1] // 512
-            for c in range(2):
-                cols = slice(first + N * c, first + N * (c + 1))
-                bank = psum.tile([P, N], F32, name="bank", bufs=8)
+        def scores(name, words, plane, dtype, pieces):
+            width = plane.shape[2]
+            per = words.shape[1] // width
+            res = keep.tile([P, width], F32, name=name)
+            first = 0
+            for n, on_scalar, tag in pieces:
+                cols = slice(first, first + n)
+                bank = psum.tile([P, n], F32, name=f"{name}_bank{first}", tag=f"bank{tag}")
                 nc.tensor.matmul_mx(out=bank[:], lhsT=q_codes[:].bitcast(FP8X4), lhsT_scale=q_scales[:],
-                                    rhs=words[:, per * N * c : per * N * (c + 1)].bitcast(dtype),
+                                    rhs=words[:, per * first : per * (first + n)].bitcast(dtype),
                                     rhs_scale=plane[:, 0, cols], start=True, stop=True)
-                if on_scalar[c]:
+                if on_scalar:
                     nc.scalar.activation(res[:, cols], bank[:], COPY)
                 else:
                     nc.vector.tensor_copy(res[:, cols], bank[:])
+                first += n
+            return res
 
         w = keep.tile([P, SLOTS], F32)
 
-        def pick_and_put(res, offsets, first):
-            n = 16 * offsets.shape[1]
-            nc.vector.tensor_copy(w[:, first : first + n], res[:].indirect(offsets[:]))
+        def pick(res, offsets, first):
+            nc.vector.tensor_copy(w[:, first : first + 16 * offsets.shape[1]], res[:].indirect(offsets[:]))
+
+        def put(first, n):
             nc.scalar.activation(page[:].indirect(put_list[:, first // 16 : (first + n) // 16]),
                                  w[:, first : first + n], COPY)
 
-        c0 = keep.tile([P, X], F32)
-        a = keep.tile([P, T], F32)
-        b = keep.tile([P, U], F32)
-        scores(c0, 0, arch_w, arch_s, FP4X4, (True, True))
-        scores(b, 0, draft_w, draft_s, FP8X4, (True, True))
-        pick_and_put(c0, arch_list, 384)
-        scores(a, 0, cache_w[:, :T], cache_s, FP4X4, (False, False))
-        scores(a, 512, cache_w[:, T:], cache_s, FP4X4, (False, False))
-        pick_and_put(b, draft_list, 256)
-        pick_and_put(a, cache_list, 0)
+        a = scores("a", cache_w, cache_s, FP4X4, ((256, True, 0), (256, False, 1), (256, True, 2), (128, False, 3), (128, False, 4)))
+        pick(a, cache_list, 0)
+        put(0, 256)
+        b = scores("b", draft_w, draft_s, FP8X4, ((512, False, 2),))
+        pick(b, draft_list, 256)
+        c0 = scores("c0", arch_w, arch_s, FP4X4, ((256, False, 5), (256, False, 6)))
+        pick(c0, arch_list, 384)
+        put(256, 256)
 
         half = SLOTS // 2
         got = keep.tile([P, SLOTS], F32)

@@ -14,10 +14,15 @@ COPY = mybir.ActivationFunctionType.Copy
 MAX = mybir.AluOpType.max
 
 P = 128
+QUADRANT = 32
+QUADRANTS = P // QUADRANT
+SCALE_ROWS = 4
+PACK = 4
+LIST_COLUMN = 16
 D, Q = 512, 128
 T, U, X, Z = 1024, 512, 512, 1024
 SLOTS = 512
-N = 256
+CACHE_SLOT, DRAFT_SLOT, ARCH_SLOT = 0, 256, 384
 FLOPS = 2 * D * Q * (T + U + X)
 
 
@@ -34,105 +39,105 @@ def tile_attend_raggedthree_three_kernel(tc, query, cache_words, cache_scales, d
             nc.sync.dma_start(tile[:], src)
             return tile
 
-        def scale_tile(name, width, loads):
-            plane = keep.tile([P, 4 // loads, width], U8, name=name, align_bytes=64)
-            nc.vector.memset(plane[:, 0, :].bitcast(I32), 0)
-            return plane
+        def scale_tile(name, tokens, per_load):
+            scales = keep.tile([P, per_load, tokens], U8, name=name, align_bytes=64)
+            nc.vector.memset(scales[:, 0, :].bitcast(I32), 0)
+            return scales
 
-        def load_scales(plane, src, first, queue):
-            groups = plane.shape[1]
-            queue.dma_start(plane[32 * first : 32 * first + 4, :, :].bitcast(I32),
-                            src[0, 4 * first : 4 * (first + groups), :].bitcast(I32).rearrange("(g r) n -> r g n", r=4))
+        def scale_loads(scales, src, queue):
+            per_load = scales.shape[1]
+            for first in range(0, QUADRANTS, per_load):
+                rows = src[0, SCALE_ROWS * first : SCALE_ROWS * (first + per_load), :]
+                queue.dma_start(scales[QUADRANT * first : QUADRANT * first + SCALE_ROWS, :, :].bitcast(I32),
+                                rows.bitcast(I32).rearrange("(g r) n -> r g n", r=SCALE_ROWS))
 
-        def load_words(name, src, nbytes):
-            words = keep.tile([P, nbytes], U8, name=name, align_bytes=64)
+        def load_words(name, src):
+            words = keep.tile([P, src.shape[1]], U8, name=name, align_bytes=64)
             nc.sync.dma_start(words[:].bitcast(I32), src.bitcast(I32))
             return words
 
-        q_raw = keep.tile([P, 4, Q], F32)
-        nc.sync.dma_start(q_raw[:], query.rearrange("(p j) q -> p j q", j=4))
-        cache_s = scale_tile("cache_s", T, 4)
-        draft_s = scale_tile("draft_s", U, 2)
-        arch_s = scale_tile("arch_s", X, 4)
-        for g in range(4):
-            load_scales(cache_s, cache_scales, g, nc.scalar)
-        cache_w = load_words("cache_w", cache_words[0], 2 * T)
-        for g in (0, 2):
-            load_scales(draft_s, draft_scales, g, nc.sync)
+        q_raw = keep.tile([P, PACK, Q], F32)
+        nc.sync.dma_start(q_raw[:], query.rearrange("(p j) q -> p j q", j=PACK))
+        cache_s = scale_tile("cache_s", T, 1)
+        arch_s = scale_tile("arch_s", X, 2)
+        draft_s = scale_tile("draft_s", U, 1)
+        scale_loads(cache_s, cache_scales, nc.scalar)
+        cache_w = load_words("cache_w", cache_words[0])
+        scale_loads(arch_s, arch_scales, nc.sync)
+        arch_w = load_words("arch_w", arch_words[0])
         cache_list = load_list("cache_list", offs)
-        draft_w = load_words("draft_w", draft_words[0].rearrange("p n t -> p (n t)"), 4 * U)
-        arch_w = load_words("arch_w", arch_words[0], 2 * X)
-        for g in range(4):
-            load_scales(arch_s, arch_scales, g, nc.sync)
+        draft_w = load_words("draft_w", draft_words[0].rearrange("p n t -> p (n t)"))
+        scale_loads(draft_s, draft_scales, nc.sync)
         put_list = load_list("put_list", offs4)
-        draft_list = load_list("draft_list", offs2)
         arch_list = load_list("arch_list", offs3)
+        draft_list = load_list("draft_list", offs2)
         get_list = load_list("get_list", offs5)
 
         page = keep.tile([P, Z], F32)
         nc.vector.memset(page[:], 0.0)
 
-        def spread_scales(plane):
-            groups = plane.shape[1]
-            for first in range(0, 4, groups):
-                for g in range(1, groups):
-                    nc.vector.tensor_copy(plane[32 * (first + g) : 32 * (first + g) + 4, 0, :].bitcast(I32),
-                                          plane[32 * first : 32 * first + 4, g, :].bitcast(I32))
-
-        q_bf = keep.tile([P, Q, 4], BF16, align_bytes=64)
+        q_bf = keep.tile([P, Q, PACK], BF16, align_bytes=64)
         q_codes = keep.tile([P, Q], U32, align_bytes=64)
         q_scales = keep.tile([P, Q], U8, align_bytes=64)
         q_halves = (slice(0, Q // 2), slice(Q // 2, Q))
-        for rows in q_halves:
-            nc.vector.tensor_copy(q_bf[:, rows, :].rearrange("p (c i) j -> p c j i", i=4),
-                                  q_raw[:, :, rows].rearrange("p j (c i) -> p c j i", i=4))
-        for rows in q_halves:
-            nc.vector.quantize_mx(out=q_codes[:, rows].bitcast(FP8X4), scales=q_scales[:, rows],
-                                  in_=q_bf[:, rows, :].rearrange("p q j -> p (q j)"))
-        spread_scales(draft_s)
+        for half in q_halves:
+            nc.vector.tensor_copy(q_bf[:, half, :].rearrange("p (c i) j -> p c j i", i=4),
+                                  q_raw[:, :, half].rearrange("p j (c i) -> p c j i", i=4))
+        for half in q_halves:
+            nc.vector.quantize_mx(out=q_codes[:, half].bitcast(FP8X4), scales=q_scales[:, half],
+                                  in_=q_bf[:, half, :].rearrange("p q j -> p (q j)"))
 
-        def scores(name, words, plane, dtype, pieces):
-            width = plane.shape[2]
-            per = words.shape[1] // width
-            res = keep.tile([P, width], F32, name=name)
+        for first in (0, 2):
+            own = QUADRANT * (first + 1)
+            nc.vector.tensor_copy(arch_s[own : own + SCALE_ROWS, 0, :].bitcast(I32),
+                                  arch_s[QUADRANT * first : QUADRANT * first + SCALE_ROWS, 1, :].bitcast(I32))
+
+        def on_scalar(dst, bank):
+            nc.scalar.activation(dst, bank, COPY)
+
+        def on_vector(dst, bank):
+            nc.vector.tensor_copy(dst, bank)
+
+        def scores(name, words, scales, dtype, pieces):
+            tokens = scales.shape[2]
+            word_bytes = words.shape[1] // tokens
+            result = keep.tile([P, tokens], F32, name=name)
             first = 0
-            for n, on_scalar, tag in pieces:
+            for n, empty, bank_number in pieces:
                 cols = slice(first, first + n)
-                bank = psum.tile([P, n], F32, name=f"{name}_bank{first}", tag=f"bank{tag}")
+                bank = psum.tile([P, n], F32, name=f"{name}_bank{first}", tag=f"bank{bank_number}")
                 nc.tensor.matmul_mx(out=bank[:], lhsT=q_codes[:].bitcast(FP8X4), lhsT_scale=q_scales[:],
-                                    rhs=words[:, per * first : per * (first + n)].bitcast(dtype),
-                                    rhs_scale=plane[:, 0, cols], start=True, stop=True)
-                if on_scalar:
-                    nc.scalar.activation(res[:, cols], bank[:], COPY)
-                else:
-                    nc.vector.tensor_copy(res[:, cols], bank[:])
+                                    rhs=words[:, word_bytes * first : word_bytes * (first + n)].bitcast(dtype),
+                                    rhs_scale=scales[:, 0, cols], start=True, stop=True)
+                empty(result[:, cols], bank[:])
                 first += n
-            return res
+            return result
 
         w = keep.tile([P, SLOTS], F32)
 
-        def pick(res, offsets, first):
-            nc.vector.tensor_copy(w[:, first : first + 16 * offsets.shape[1]], res[:].indirect(offsets[:]))
+        def pick(result, offsets, first):
+            n = LIST_COLUMN * offsets.shape[1]
+            nc.vector.tensor_copy(w[:, first : first + n], result[:].indirect(offsets[:]))
 
-        def put(first, n):
-            nc.scalar.activation(page[:].indirect(put_list[:, first // 16 : (first + n) // 16]),
-                                 w[:, first : first + n], COPY)
+        def put(first, end):
+            nc.scalar.activation(page[:].indirect(put_list[:, first // LIST_COLUMN : end // LIST_COLUMN]),
+                                 w[:, first:end], COPY)
 
-        a = scores("a", cache_w, cache_s, FP4X4, ((256, True, 0), (256, False, 1), (256, True, 2), (128, False, 3), (128, False, 4)))
-        pick(a, cache_list, 0)
-        put(0, 256)
-        b = scores("b", draft_w, draft_s, FP8X4, ((512, False, 2),))
-        pick(b, draft_list, 256)
-        c0 = scores("c0", arch_w, arch_s, FP4X4, ((256, False, 5), (256, False, 6)))
-        pick(c0, arch_list, 384)
-        put(256, 256)
+        a = scores("a", cache_w, cache_s, FP4X4,
+                   ((256, on_scalar, 0), (256, on_vector, 1), (256, on_scalar, 2), (128, on_vector, 3), (128, on_vector, 4)))
+        c0 = scores("c0", arch_w, arch_s, FP4X4, ((256, on_scalar, 1), (256, on_scalar, 0)))
+        pick(a, cache_list, CACHE_SLOT)
+        put(CACHE_SLOT, DRAFT_SLOT)
+        pick(c0, arch_list, ARCH_SLOT)
+        b = scores("b", draft_w, draft_s, FP8X4, ((512, on_vector, 2),))
+        pick(b, draft_list, DRAFT_SLOT)
+        put(DRAFT_SLOT, SLOTS)
 
-        half = SLOTS // 2
+        middle = SLOTS // 2
         got = keep.tile([P, SLOTS], F32)
-        res = keep.tile([P, SLOTS], F32)
-        nc.vector.tensor_copy(got[:, :half], page[:].indirect(get_list[:, : half // 16]))
-        nc.scalar.activation(got[:, half:], page[:].indirect(get_list[:, half // 16 :]), COPY)
-        for h in range(2):
-            cols = slice(h * half, (h + 1) * half)
-            nc.vector.tensor_tensor(res[:, cols], got[:, cols], w[:, cols], MAX)
-            nc.sync.dma_start(out[:, cols], res[:, cols])
+        larger = keep.tile([P, SLOTS], F32)
+        nc.vector.tensor_copy(got[:, :middle], page[:].indirect(get_list[:, : middle // LIST_COLUMN]))
+        nc.scalar.activation(got[:, middle:], page[:].indirect(get_list[:, middle // LIST_COLUMN :]), COPY)
+        for cols in (slice(0, middle), slice(middle, SLOTS)):
+            nc.vector.tensor_tensor(larger[:, cols], got[:, cols], w[:, cols], MAX)
+            nc.sync.dma_start(out[:, cols], larger[:, cols])

from contextlib import ExitStack

import concourse.mybir as mybir

F32 = mybir.dt.float32
BF16 = mybir.dt.bfloat16
I32 = mybir.dt.int32
U32 = mybir.dt.uint32
U16 = mybir.dt.uint16
U8 = mybir.dt.uint8
FP8X4 = mybir.dt.float8_e4m3fn_x4
FP4X4 = mybir.dt.float4_e2m1fn_x4
COPY = mybir.ActivationFunctionType.Copy
MAX = mybir.AluOpType.max

P = 128
QUADRANT = 32
QUADRANTS = P // QUADRANT
SCALE_ROWS = 4
PACK = 4
LIST_COLUMN = 16
D, Q = 512, 128
T, U, X, Z = 1024, 512, 512, 1024
SLOTS = 512
CACHE_SLOT, DRAFT_SLOT, ARCH_SLOT = 0, 256, 384
FLOPS = 2 * D * Q * (T + U + X)


def tile_attend_raggedthree_three_kernel(tc, query, cache_words, cache_scales, draft_words, draft_scales,
                                          arch_words, arch_scales, offs, offs2, offs3, offs4, offs5, out):
    nc = tc.nc
    with ExitStack() as ctx:
        lists = ctx.enter_context(tc.tile_pool(name="lists", bufs=1))
        keep = ctx.enter_context(tc.tile_pool(name="keep", bufs=1))
        psum = ctx.enter_context(tc.psum_pool(name="psum", bufs=1))

        def load_list(name, src):
            tile = lists.tile(list(src.shape), U16, name=name)
            nc.sync.dma_start(tile[:], src)
            return tile

        def scale_tile(name, tokens, per_load):
            scales = keep.tile([P, per_load, tokens], U8, name=name, align_bytes=64)
            nc.vector.memset(scales[:, 0, :].bitcast(I32), 0)
            return scales

        def scale_loads(scales, src, queue):
            per_load = scales.shape[1]
            for first in range(0, QUADRANTS, per_load):
                rows = src[0, SCALE_ROWS * first : SCALE_ROWS * (first + per_load), :]
                queue.dma_start(scales[QUADRANT * first : QUADRANT * first + SCALE_ROWS, :, :].bitcast(I32),
                                rows.bitcast(I32).rearrange("(g r) n -> r g n", r=SCALE_ROWS))

        def load_words(name, src):
            words = keep.tile([P, src.shape[1]], U8, name=name, align_bytes=64)
            nc.sync.dma_start(words[:].bitcast(I32), src.bitcast(I32))
            return words

        q_raw = keep.tile([P, PACK, Q], F32)
        nc.sync.dma_start(q_raw[:], query.rearrange("(p j) q -> p j q", j=PACK))
        cache_s = scale_tile("cache_s", T, 1)
        arch_s = scale_tile("arch_s", X, 2)
        draft_s = scale_tile("draft_s", U, 1)
        scale_loads(cache_s, cache_scales, nc.scalar)
        cache_w = load_words("cache_w", cache_words[0])
        scale_loads(arch_s, arch_scales, nc.sync)
        arch_w = load_words("arch_w", arch_words[0])
        cache_list = load_list("cache_list", offs)
        draft_w = load_words("draft_w", draft_words[0].rearrange("p n t -> p (n t)"))
        scale_loads(draft_s, draft_scales, nc.sync)
        put_list = load_list("put_list", offs4)
        arch_list = load_list("arch_list", offs3)
        draft_list = load_list("draft_list", offs2)
        get_list = load_list("get_list", offs5)

        page = keep.tile([P, Z], F32)
        nc.vector.memset(page[:], 0.0)

        q_bf = keep.tile([P, Q, PACK], BF16, align_bytes=64)
        q_codes = keep.tile([P, Q], U32, align_bytes=64)
        q_scales = keep.tile([P, Q], U8, align_bytes=64)
        q_halves = (slice(0, Q // 2), slice(Q // 2, Q))
        for half in q_halves:
            nc.vector.tensor_copy(q_bf[:, half, :].rearrange("p (c i) j -> p c j i", i=4),
                                  q_raw[:, :, half].rearrange("p j (c i) -> p c j i", i=4))
        for half in q_halves:
            nc.vector.quantize_mx(out=q_codes[:, half].bitcast(FP8X4), scales=q_scales[:, half],
                                  in_=q_bf[:, half, :].rearrange("p q j -> p (q j)"))

        for first in (0, 2):
            own = QUADRANT * (first + 1)
            nc.vector.tensor_copy(arch_s[own : own + SCALE_ROWS, 0, :].bitcast(I32),
                                  arch_s[QUADRANT * first : QUADRANT * first + SCALE_ROWS, 1, :].bitcast(I32))

        def on_scalar(dst, bank):
            nc.scalar.activation(dst, bank, COPY)

        def on_vector(dst, bank):
            nc.vector.tensor_copy(dst, bank)

        def scores(name, words, scales, dtype, pieces):
            tokens = scales.shape[2]
            word_bytes = words.shape[1] // tokens
            result = keep.tile([P, tokens], F32, name=name)
            first = 0
            for n, empty, bank_number in pieces:
                cols = slice(first, first + n)
                bank = psum.tile([P, n], F32, name=f"{name}_bank{first}", tag=f"bank{bank_number}")
                nc.tensor.matmul_mx(out=bank[:], lhsT=q_codes[:].bitcast(FP8X4), lhsT_scale=q_scales[:],
                                    rhs=words[:, word_bytes * first : word_bytes * (first + n)].bitcast(dtype),
                                    rhs_scale=scales[:, 0, cols], start=True, stop=True)
                empty(result[:, cols], bank[:])
                first += n
            return result

        w = keep.tile([P, SLOTS], F32)

        def pick(result, offsets, first):
            n = LIST_COLUMN * offsets.shape[1]
            nc.vector.tensor_copy(w[:, first : first + n], result[:].indirect(offsets[:]))

        def put(first, end):
            nc.scalar.activation(page[:].indirect(put_list[:, first // LIST_COLUMN : end // LIST_COLUMN]),
                                 w[:, first:end], COPY)

        a = scores("a", cache_w, cache_s, FP4X4,
                   ((256, on_scalar, 0), (256, on_vector, 1), (256, on_scalar, 2), (128, on_vector, 3), (128, on_vector, 4)))
        c0 = scores("c0", arch_w, arch_s, FP4X4, ((256, on_scalar, 1), (256, on_scalar, 0)))
        pick(a, cache_list, CACHE_SLOT)
        put(CACHE_SLOT, DRAFT_SLOT)
        pick(c0, arch_list, ARCH_SLOT)
        b = scores("b", draft_w, draft_s, FP8X4, ((512, on_vector, 2),))
        pick(b, draft_list, DRAFT_SLOT)
        put(DRAFT_SLOT, SLOTS)

        middle = SLOTS // 2
        got = keep.tile([P, SLOTS], F32)
        larger = keep.tile([P, SLOTS], F32)
        nc.vector.tensor_copy(got[:, :middle], page[:].indirect(get_list[:, : middle // LIST_COLUMN]))
        nc.scalar.activation(got[:, middle:], page[:].indirect(get_list[:, middle // LIST_COLUMN :]), COPY)
        for cols in (slice(0, middle), slice(middle, SLOTS)):
            nc.vector.tensor_tensor(larger[:, cols], got[:, cols], w[:, cols], MAX)
            nc.sync.dma_start(out[:, cols], larger[:, cols])
